import numpy as np
import ml_dtypes


def mxq(x, axis, fmt="e4m3"):
    dtype, down = {"e4m3": (ml_dtypes.float8_e4m3fn, 7), "e5m2": (ml_dtypes.float8_e5m2, 14)}[fmt]
    v = np.moveaxis(np.asarray(x, np.float32).astype(ml_dtypes.bfloat16).astype(np.float64), axis, -1)
    blocks = v.reshape(v.shape[:-1] + (-1, 32))
    amax = np.abs(blocks).max(-1, keepdims=True)
    byte = np.maximum(np.where(amax > 0, np.frexp(amax)[1] - 1 + 127, 0) - down, 1)
    scale = np.exp2(byte - 127.0)
    codes = (blocks / scale).astype(np.float32).astype(dtype).astype(np.float64)
    return np.moveaxis((codes * scale).reshape(v.shape), -1, axis)


WIDE = False


def mx_kscale(k):
    if not WIDE:
        return np.ones(k)
    levels = np.array([30, -30])
    if k % 512:
        return np.exp2(np.random.permutation(np.resize(levels, k // 32))).repeat(32)
    a = np.empty((k // 512, 16))
    for p in range(k // 512):
        a[p, :8] = np.random.permutation(np.resize(levels, 8))
        for g in range(8):
            far = levels[np.abs(levels - a[p, g]) >= 10]
            a[p, g + 8] = far[np.random.randint(len(far))]
    return np.exp2(a.ravel()).repeat(32)


def f64(x):
    return np.asarray(x).astype(np.float64)


def striped(idx):
    return np.tile(np.asarray(idx).reshape(-1, 16).T, (8, 1)).astype(np.uint16)


def unstriped(offs):
    return offs[:16].T.reshape(-1).astype(np.int64)


E2M1 = np.array([0.0, 0.5, 1.0, 1.5, 2.0, 3.0, 4.0, 6.0, -0.0, -0.5, -1.0, -1.5, -2.0, -3.0, -4.0, -6.0])


def pack_weight(w, fmt):
    k, n = w.shape
    w = f64(np.asarray(w, np.float32).astype(ml_dtypes.bfloat16)).reshape(k // 32, 32, n)
    amax = np.abs(w).max(1)
    if fmt in ("e4m3", "e5m2"):
        byte = np.frexp(amax)[1] - 1 + 127 - (7 if fmt == "e4m3" else 14)
    else:
        mant, ex = np.frexp(amax / 6.0)
        byte = np.where(mant > 0.5, ex, ex - 1) + 127
    byte = np.clip(np.where(amax > 0, byte, 1), 1, 254)
    scaled = (w * np.exp2(127.0 - byte)[:, None, :]).reshape(k, n).astype(np.float32)
    by_word = np.ascontiguousarray(scaled.reshape(k // 512, 128, 4, n).transpose(0, 1, 3, 2))
    if fmt in ("e4m3", "e5m2"):
        words = by_word.astype(ml_dtypes.float8_e4m3fn if fmt == "e4m3" else ml_dtypes.float8_e5m2).view(np.uint8)
    else:
        c = by_word.astype(ml_dtypes.float4_e2m1fn).view(np.uint8) & 0xF
        words = (c[..., 0::2] | (c[..., 1::2] << 4)).reshape(k // 512, 128, 2 * n)
    return np.ascontiguousarray(words), np.ascontiguousarray(byte.astype(np.uint8).reshape(k // 512, 16, n))


def unpack_weight(words, scales, fmt):
    g, _, n = scales.shape
    words = np.ascontiguousarray(words).reshape(g, 128, n, -1)
    if fmt in ("e4m3", "e5m2"):
        vals = words.view(ml_dtypes.float8_e4m3fn if fmt == "e4m3" else ml_dtypes.float8_e5m2).astype(np.float64)
    else:
        nib = np.empty((g, 128, n, 4), np.uint8)
        nib[..., 0::2] = words & 0xF
        nib[..., 1::2] = words >> 4
        vals = E2M1[nib]
    vals = vals * np.repeat(np.exp2(scales.astype(np.float64) - 127.0), 8, axis=1)[..., None]
    return vals.transpose(0, 1, 3, 2).reshape(g * 512, n)


def bf(x):
    return np.asarray(x, np.float32).astype(ml_dtypes.bfloat16)


def planes(Y):
    r, m = Y.shape
    b = f64(bf(Y)).reshape(r // 32, 32, m)
    amax = np.abs(b).max(1)
    byte = np.clip(np.where(amax > 0, np.frexp(amax)[1] - 1 + 127 - 7, 1), 1, 254)
    codes = (b * np.exp2(127.0 - byte)[:, None, :]).reshape(r, m).astype(np.float32).astype(ml_dtypes.float8_e4m3fn).view(np.uint8)
    words = codes.reshape(r // 512, 128, 4, m).transpose(0, 1, 3, 2)
    return np.ascontiguousarray(words), np.ascontiguousarray(byte.astype(np.uint8).reshape(r // 512, 16, m))


K, T, J, R, C, O, N, L, E = 512, 1024, 256, 512, 512, 256, 512, 512, 1024


def setup_inputs():
    n = np.random.standard_normal
    idx = np.random.permutation(T)[:J]
    idx2 = np.random.permutation(C)[:J]
    idx3 = np.random.permutation(C)[:J]
    idx4 = np.random.permutation(C)[:O]
    idx5 = np.random.permutation(E)[:O]
    fk = mx_kscale(K)
    fr = mx_kscale(R)
    fl = mx_kscale(L)
    xtp = pack_weight(n((K, T)) / fk[:, None], "e4m3")
    wp = pack_weight(n((K, R)) * 1 / np.sqrt(K) * fk[:, None] * fr, "e2m1")
    w2p = pack_weight(n((K, R)) * 1 / np.sqrt(K) * fk[:, None] * fr, "e5m2")
    wbp = pack_weight(n((R, N)) * 1 / np.sqrt(R) / fr[:, None], "e5m2")
    sxp = pack_weight(n((L, O)) / fl[:, None], "e2m1")
    wsp = pack_weight(n((L, N)) * 1 / np.sqrt(L) * fl[:, None], "e5m2")
    return {
        "xt_words": xtp[0],
        "xt_scales": xtp[1],
        "w_words": wp[0],
        "w_scales": wp[1],
        "w2_words": w2p[0],
        "w2_scales": w2p[1],
        "wb_words": wbp[0],
        "wb_scales": wbp[1],
        "sx_words": sxp[0],
        "sx_scales": sxp[1],
        "ws_words": wsp[0],
        "ws_scales": wsp[1],
        "tz": (n((N, E))).astype(np.float32),
        "offs": striped(idx),
        "offs2": striped(idx2),
        "offs3": striped(idx3),
        "offs4": striped(idx4),
        "offs5": striped(idx5),
    }


def reference(xt_words, xt_scales, w_words, w_scales, w2_words, w2_scales, wb_words, wb_scales, sx_words, sx_scales, ws_words, ws_scales, tz, offs, offs2, offs3, offs4, offs5):
    idx = unstriped(offs)
    idx2 = unstriped(offs2)
    idx3 = unstriped(offs3)
    idx4 = unstriped(offs4)
    idx5 = unstriped(offs5)
    xtu = unpack_weight(xt_words, xt_scales, "e4m3")
    wu = unpack_weight(w_words, w_scales, "e2m1")
    w2u = unpack_weight(w2_words, w2_scales, "e5m2")
    wbu = unpack_weight(wb_words, wb_scales, "e5m2")
    sxu = unpack_weight(sx_words, sx_scales, "e2m1")
    wsu = unpack_weight(ws_words, ws_scales, "e5m2")
    xtidxg = xtu[:, idx]
    a = wu.T @ xtidxg
    b = w2u.T @ xtidxg
    pw = np.zeros((R, C))
    pw[:, idx2] = a
    pv = np.zeros((R, C))
    pv[:, idx3] = b
    pg = pw + pv
    hid = pg[:, idx4]
    hidq = mxq(hid, 0, "e4m3")
    p = wbu.T @ hidq + wsu.T @ sxu
    y = p + f64(tz)[:, idx5]
    words, scales = planes(y)
    return y, words, scales

@@ -1,0 +1,225 @@
+from contextlib import ExitStack
+
+import concourse.mybir as mybir
+
+K, T, J, R, C, O, N, L, E = 512, 1024, 256, 512, 512, 256, 512, 512, 1024
+FLOPS = 2 * (2 * K * R * J + R * N * O + L * N * O)
+
+F32 = mybir.dt.float32
+BF16 = mybir.dt.bfloat16
+I32 = mybir.dt.int32
+U32 = mybir.dt.uint32
+U16 = mybir.dt.uint16
+U8 = mybir.dt.uint8
+E4M3 = mybir.dt.float8_e4m3fn_x4
+E5M2 = mybir.dt.float8_e5m2_x4
+E2M1 = mybir.dt.float4_e2m1fn_x4
+ADD = mybir.AluOpType.add
+COPY = mybir.ActivationFunctionType.Copy
+
+P = 128
+PACK = 4
+HALF = O // 2
+HCOL = HALF // 16
+
+
+def load_scales(nc, dst, src):
+    for q in range(4):
+        nc.sync.dma_start(dst[32 * q : 32 * q + 4, :].bitcast(I32), src[0, 4 * q : 4 * q + 4, :].bitcast(I32))
+
+
+def deal(nc, dst, src):
+    nc.vector.tensor_copy(dst.rearrange("p (t m) -> p m t", t=PACK), src.rearrange("p (m t) -> p m t", t=PACK))
+
+
+def woven(dst, src):
+    return dst.rearrange("p (c i t) -> p c t i", i=4, t=PACK), src.rearrange("p t (c i) -> p c t i", i=4)
+
+
+def tile_list_twow_shared_skip_tabled_pl_kernel(
+    tc, xt_words, xt_scales, w_words, w_scales, w2_words, w2_scales, wb_words, wb_scales,
+    sx_words, sx_scales, ws_words, ws_scales, tz, offs, offs2, offs3, offs4, offs5, out_0, out_1, out_2,
+):
+    nc = tc.nc
+    with ExitStack() as ctx:
+        lists = ctx.enter_context(tc.tile_pool(name="lists", bufs=1))
+        sb = ctx.enter_context(tc.tile_pool(name="sb", bufs=1))
+        psum = ctx.enter_context(tc.psum_pool(name="psum", bufs=1))
+
+        def tile(name, shape, dtype, tag=None):
+            return sb.tile(shape, dtype, name=name, tag=tag or name, align_bytes=64)
+
+        def words(src):
+            return src[0].rearrange("p c r -> p (c r)").bitcast(I32)
+
+        l1 = lists.tile([P, J // 16], U16, name="l1")
+        l2 = lists.tile([P, J // 16], U16, name="l2")
+        l3 = lists.tile([P, J // 16], U16, name="l3")
+        l4 = lists.tile([P, O // 16], U16, name="l4")
+        l5 = lists.tile([P, O // 16], U16, name="l5")
+
+        xs = tile("xs", [P, T], U8)
+        w_s = tile("w_s", [P, R], U8)
+        w2_s = tile("w2_s", [P, R], U8)
+        late_s = tile("late_s", [P, 2 * N], U8, tag="hid_rows")
+        sx_s = tile("sx_s", [P, O], U8)
+        for plane in (xs, w_s, w2_s):
+            nc.vector.memset(plane[:].bitcast(I32), 0)
+        for plane in (late_s, sx_s):
+            nc.gpsimd.memset(plane[:].bitcast(I32), 0)
+        pw = [tile("pw%d" % i, [P, C], F32) for i in range(3)]
+        pv = [tile("pv%d" % i, [P, C], F32) for i in range(2)]
+        for board in (pw[0], pw[1], pv[0], pv[1], pw[2]):
+            nc.vector.memset(board[:], 0.0)
+
+        xw = tile("xw", [P, T], I32)
+        w_w = tile("w_w", [P, 2 * R], U8)
+        w2_w = tile("w2_w", [P, R], I32)
+        wb_w = tile("wb_w", [P, N], I32, tag="vstage2")
+        ws_w = tile("ws_w", [P, N], I32, tag="vstage3")
+        sx_w = tile("sx_w", [P, 2 * O], U8)
+        tzt = [tile("tz%d" % t, [P, E], F32) for t in range(PACK)]
+        tz_rows = tz.rearrange("(p t) e -> p t e", t=PACK)
+
+        load_scales(nc, xs, xt_scales)
+        nc.sync.dma_start(xw[:], words(xt_words))
+        nc.sync.dma_start(l1[:], offs)
+        nc.sync.dma_start(w_w[:].bitcast(I32), w_words[0].bitcast(I32))
+        load_scales(nc, w_s, w_scales)
+        nc.sync.dma_start(l2[:], offs2)
+        nc.sync.dma_start(w2_w[:], words(w2_words))
+        load_scales(nc, w2_s, w2_scales)
+        nc.sync.dma_start(l3[:], offs3)
+        nc.sync.dma_start(wb_w[:], words(wb_words))
+        nc.sync.dma_start(ws_w[:], words(ws_words))
+        load_scales(nc, late_s[:, 0:N], wb_scales)
+        load_scales(nc, late_s[:, N : 2 * N], ws_scales)
+        nc.sync.dma_start(l4[:], offs4)
+        nc.sync.dma_start(sx_w[:].bitcast(I32), sx_words[0].bitcast(I32))
+        load_scales(nc, sx_s, sx_scales)
+        nc.sync.dma_start(l5[:], offs5)
+        for t in range(PACK):
+            nc.sync.dma_start(tzt[t][:], tz_rows[:, t, :])
+
+        xg_s = tile("xg_s", [P, J], U8)
+        xg_w = tile("xg_w", [P, J], U32)
+        nc.vector.tensor_copy(xg_s[:], xs[:].indirect(l1[:]))
+        nc.vector.tensor_copy(xg_w[:], xw[:].bitcast(U32).indirect(l1[:]))
+        wd_w = tile("wd_w", [P, 2 * R], U8)
+        wd_s = tile("wd_s", [P, R], U8)
+        deal(nc, wd_w[:].bitcast(U16), w_w[:].bitcast(U16))
+        deal(nc, wd_s[:], w_s[:])
+        w2d_w = tile("w2d_w", [P, R], I32)
+        w2d_s = tile("w2d_s", [P, R], U8)
+        deal(nc, w2d_w[:], w2_w[:])
+        deal(nc, w2d_s[:], w2_s[:])
+
+        def first(t, bank):
+            acc = psum.tile([P, J], F32, name="a%d" % t, tag=bank)
+            nc.tensor.matmul_mx(
+                acc[:], lhsT=wd_w[:, 2 * P * t : 2 * P * (t + 1)].bitcast(E2M1), lhsT_scale=wd_s[:, P * t : P * (t + 1)],
+                rhs=xg_w[:].bitcast(E4M3), rhs_scale=xg_s[:], start=True, stop=True)
+            return acc
+
+        def second(t, bank):
+            acc = psum.tile([P, J], F32, name="b%d" % t, tag=bank)
+            nc.tensor.matmul_mx(
+                acc[:], lhsT=w2d_w[:, P * t : P * (t + 1)].bitcast(E5M2), lhsT_scale=w2d_s[:, P * t : P * (t + 1)],
+                rhs=xg_w[:].bitcast(E4M3), rhs_scale=xg_s[:], start=True, stop=True)
+            return acc
+
+        def put_scalar(acc, board, offsets, name, tag):
+            st = tile(name, [P, J], F32, tag=tag)
+            nc.scalar.activation(st[:], acc[:], COPY)
+            nc.scalar.activation(board[:].indirect(offsets[:]), st[:], COPY)
+
+        def put_vector(acc, board, offsets, name, tag):
+            st = tile(name, [P, J], F32, tag=tag)
+            nc.vector.tensor_copy(st[:], acc[:])
+            nc.vector.tensor_copy(board[:].indirect(offsets[:]), st[:])
+
+        pg = [tile("pg%d" % t, [P, C], F32) for t in range(PACK)]
+
+        a0 = first(0, "bank0")
+        a1 = first(1, "bank1")
+        put_scalar(a0, pw[0], l2, "sa0", "sstage0")
+        put_vector(a1, pw[1], l2, "sa1", "vstage0")
+        b0 = second(0, "bank2")
+        b1 = second(1, "bank3")
+        put_scalar(b0, pv[0], l3, "sb0", "sstage1")
+        put_vector(b1, pv[1], l3, "sb1", "vstage1")
+        nc.gpsimd.tensor_tensor(pg[0][:], pw[0][:], pv[0][:], ADD)
+        nc.gpsimd.tensor_tensor(pg[1][:], pw[1][:], pv[1][:], ADD)
+
+        wbd_w = tile("wbd_w", [P, N], I32)
+        wsd_w = tile("wsd_w", [P, N], I32)
+        lated_s = tile("lated_s", [P, 2 * N], U8)
+        deal(nc, wbd_w[:], wb_w[:])
+        deal(nc, wsd_w[:], ws_w[:])
+        nc.vector.tensor_copy(
+            lated_s[:].rearrange("p (g t m) -> p g m t", g=2, t=PACK),
+            late_s[:].rearrange("p (g m t) -> p g m t", g=2, t=PACK))
+
+        a2 = first(2, "bank2")
+        b2 = second(2, "bank1")
+        put_scalar(a2, pw[2], l2, "sa2", "sstage0")
+        put_vector(b2, pv[0], l3, "sb2", "vstage2")
+        hid_rows = tile("hid_rows", [P, PACK, O], BF16)
+        for t in (0, 1):
+            nc.scalar.activation(hid_rows[:, t, :], pg[t][:].indirect(l4[:]), COPY)
+        nc.gpsimd.tensor_tensor(pg[2][:], pw[2][:], pv[0][:], ADD)
+        a3 = first(3, "bank0")
+        b3 = second(3, "bank3")
+
+        acc_p = [psum.tile([P, PACK, HALF], F32, name="p%d" % h) for h in range(2)]
+        for h in range(2):
+            for t in range(PACK):
+                nc.tensor.matmul_mx(
+                    acc_p[h][:, t, :], lhsT=wsd_w[:, P * t : P * (t + 1)].bitcast(E5M2),
+                    lhsT_scale=lated_s[:, N + P * t : N + P * (t + 1)],
+                    rhs=sx_w[:, 2 * HALF * h : 2 * HALF * (h + 1)].bitcast(E2M1),
+                    rhs_scale=sx_s[:, HALF * h : HALF * (h + 1)], start=(t == 0), stop=False)
+
+        put_scalar(a3, pw[1], l2, "sa3", "sstage1")
+        put_vector(b3, pv[1], l3, "sb3", "vstage3")
+        nc.scalar.activation(hid_rows[:, 2, :], pg[2][:].indirect(l4[:]), COPY)
+        nc.vector.tensor_tensor(pg[3][:], pw[1][:], pv[1][:], ADD)
+
+        tzg = [tile("tzg%d" % h, [P, PACK, HALF], F32) for h in range(2)]
+        for h in range(2):
+            for t in range(PACK):
+                nc.scalar.activation(tzg[h][:, t, :], tzt[t][:].indirect(l5[:, HCOL * h : HCOL * (h + 1)]), COPY)
+
+        for h in range(2):
+            nc.vector.tensor_copy(hid_rows[:, 3, HALF * h : HALF * (h + 1)], pg[3][:].indirect(l4[:, HCOL * h : HCOL * (h + 1)]))
+        hid_b = [tile("hid_b%d" % h, [P, PACK * HALF], BF16) for h in range(2)]
+        hid_w = [tile("hid_w%d" % h, [P, HALF], U32) for h in range(2)]
+        hid_s = [tile("hid_s%d" % h, [P, HALF], U8) for h in range(2)]
+        for h in range(2):
+            nc.vector.tensor_copy(*woven(hid_b[h][:], hid_rows[:, :, HALF * h : HALF * (h + 1)]))
+        for h in range(2):
+            nc.vector.quantize_mx(hid_w[h][:].bitcast(E4M3), hid_s[h][:], hid_b[h][:])
+        for h in range(2):
+            for t in range(PACK):
+                nc.tensor.matmul_mx(
+                    acc_p[h][:, t, :], lhsT=wbd_w[:, P * t : P * (t + 1)].bitcast(E5M2),
+                    lhsT_scale=lated_s[:, P * t : P * (t + 1)],
+                    rhs=hid_w[h][:].bitcast(E4M3), rhs_scale=hid_s[h][:], start=False, stop=(t == PACK - 1))
+
+        y = [tile("y%d" % h, [P, PACK, HALF], F32) for h in range(2)]
+        y_b = [tile("y_b%d" % h, [P, PACK * HALF], BF16) for h in range(2)]
+        y_w = [tile("y_w%d" % h, [P, HALF], I32) for h in range(2)]
+        y_s = tile("y_s", [P, O], U8)
+        out_rows = out_0.rearrange("(p t) o -> p t o", t=PACK)
+        out_words = words(out_1)
+        for h in range(2):
+            nc.vector.tensor_tensor(y[h][:], acc_p[h][:], tzg[h][:], ADD)
+            nc.sync.dma_start(out_rows[:, :, HALF * h : HALF * (h + 1)], y[h][:])
+        nc.scalar.copy(*woven(y_b[0][:], y[0][:]))
+        nc.vector.tensor_copy(*woven(y_b[1][:], y[1][:]))
+        for h in range(2):
+            nc.vector.quantize_mx(y_w[h][:].bitcast(E4M3), y_s[:, HALF * h : HALF * (h + 1)], y_b[h][:])
+            nc.sync.dma_start(out_words[:, HALF * h : HALF * (h + 1)], y_w[h][:])
+        for q in range(4):
+            queue = nc.scalar if q % 2 == 0 else nc.sync
+            queue.dma_start(out_2[0, 4 * q : 4 * q + 4, :].bitcast(I32), y_s[32 * q : 32 * q + 4, :].bitcast(I32))

@@ -23,13 +23,18 @@ HALF = O // 2
 HCOL = HALF // 16
 
 
-def load_scales(nc, dst, src):
+def load_scales(queue, dst, src):
     for q in range(4):
-        nc.sync.dma_start(dst[32 * q : 32 * q + 4, :].bitcast(I32), src[0, 4 * q : 4 * q + 4, :].bitcast(I32))
+        queue.dma_start(dst[32 * q : 32 * q + 4, :].bitcast(I32), src[0, 4 * q : 4 * q + 4, :].bitcast(I32))
 
 
-def deal(nc, dst, src):
-    nc.vector.tensor_copy(dst.rearrange("p (t m) -> p m t", t=PACK), src.rearrange("p (m t) -> p m t", t=PACK))
+def dealt(dst, src, run):
+    return (dst.rearrange("p (t c i) -> p c t i", t=PACK, i=run), src.rearrange("p (c i t) -> p c t i", t=PACK, i=run))
+
+
+def dealt2(dst, src, run):
+    return (dst.rearrange("p (g t c i) -> p g c t i", g=2, t=PACK, i=run),
+            src.rearrange("p (g c i t) -> p g c t i", g=2, t=PACK, i=run))
 
 
 def woven(dst, src):
@@ -61,58 +66,57 @@ def tile_list_twow_shared_skip_tabled_pl_kernel(
         xs = tile("xs", [P, T], U8)
         w_s = tile("w_s", [P, R], U8)
         w2_s = tile("w2_s", [P, R], U8)
-        late_s = tile("late_s", [P, 2 * N], U8, tag="hid_rows")
+        late_s = tile("late_s", [P, 2 * N], U8, tag="vstage3")
         sx_s = tile("sx_s", [P, O], U8)
-        for plane in (xs, w_s, w2_s):
-            nc.vector.memset(plane[:].bitcast(I32), 0)
-        for plane in (late_s, sx_s):
+        for plane in (w_s, xs, w2_s, late_s, sx_s):
             nc.gpsimd.memset(plane[:].bitcast(I32), 0)
         pw = [tile("pw%d" % i, [P, C], F32) for i in range(3)]
-        pv = [tile("pv%d" % i, [P, C], F32) for i in range(2)]
-        for board in (pw[0], pw[1], pv[0], pv[1], pw[2]):
+        pv = [tile("pv%d" % i, [P, C], F32) for i in range(3)]
+        for board in (pw[0], pw[1], pw[2]):
             nc.vector.memset(board[:], 0.0)
+        for board in (pv[0], pv[2], pv[1]):
+            nc.gpsimd.memset(board[:], 0.0)
 
         xw = tile("xw", [P, T], I32)
         w_w = tile("w_w", [P, 2 * R], U8)
         w2_w = tile("w2_w", [P, R], I32)
-        wb_w = tile("wb_w", [P, N], I32, tag="vstage2")
-        ws_w = tile("ws_w", [P, N], I32, tag="vstage3")
+        late_w = tile("late_w", [P, 2 * N], I32, tag="vstage1")
         sx_w = tile("sx_w", [P, 2 * O], U8)
         tzt = [tile("tz%d" % t, [P, E], F32) for t in range(PACK)]
         tz_rows = tz.rearrange("(p t) e -> p t e", t=PACK)
 
-        load_scales(nc, xs, xt_scales)
-        nc.sync.dma_start(xw[:], words(xt_words))
         nc.sync.dma_start(l1[:], offs)
-        nc.sync.dma_start(w_w[:].bitcast(I32), w_words[0].bitcast(I32))
-        load_scales(nc, w_s, w_scales)
         nc.sync.dma_start(l2[:], offs2)
-        nc.sync.dma_start(w2_w[:], words(w2_words))
-        load_scales(nc, w2_s, w2_scales)
         nc.sync.dma_start(l3[:], offs3)
-        nc.sync.dma_start(wb_w[:], words(wb_words))
-        nc.sync.dma_start(ws_w[:], words(ws_words))
-        load_scales(nc, late_s[:, 0:N], wb_scales)
-        load_scales(nc, late_s[:, N : 2 * N], ws_scales)
+        load_scales(nc.sync, w_s, w_scales)
+        nc.sync.dma_start(xw[:], words(xt_words))
+        nc.sync.dma_start(w_w[:].bitcast(I32), w_words[0].bitcast(I32))
+        load_scales(nc.sync, xs, xt_scales)
+        load_scales(nc.sync, w2_s, w2_scales)
+        nc.sync.dma_start(w2_w[:], words(w2_words))
+        nc.sync.dma_start(late_w[:, 0:N], words(wb_words))
+        nc.sync.dma_start(late_w[:, N : 2 * N], words(ws_words))
         nc.sync.dma_start(l4[:], offs4)
+        load_scales(nc.sync, late_s[:, 0:N], wb_scales)
+        load_scales(nc.sync, late_s[:, N : 2 * N], ws_scales)
         nc.sync.dma_start(sx_w[:].bitcast(I32), sx_words[0].bitcast(I32))
-        load_scales(nc, sx_s, sx_scales)
+        load_scales(nc.sync, sx_s, sx_scales)
         nc.sync.dma_start(l5[:], offs5)
         for t in range(PACK):
             nc.sync.dma_start(tzt[t][:], tz_rows[:, t, :])
 
         xg_s = tile("xg_s", [P, J], U8)
         xg_w = tile("xg_w", [P, J], U32)
-        nc.vector.tensor_copy(xg_s[:], xs[:].indirect(l1[:]))
         nc.vector.tensor_copy(xg_w[:], xw[:].bitcast(U32).indirect(l1[:]))
+        nc.vector.tensor_copy(xg_s[:], xs[:].indirect(l1[:]))
         wd_w = tile("wd_w", [P, 2 * R], U8)
         wd_s = tile("wd_s", [P, R], U8)
-        deal(nc, wd_w[:].bitcast(U16), w_w[:].bitcast(U16))
-        deal(nc, wd_s[:], w_s[:])
+        nc.vector.tensor_copy(*dealt(wd_w[:].bitcast(U16), w_w[:].bitcast(U16), 8))
+        nc.vector.tensor_copy(*dealt(wd_s[:], w_s[:], 16))
         w2d_w = tile("w2d_w", [P, R], I32)
         w2d_s = tile("w2d_s", [P, R], U8)
-        deal(nc, w2d_w[:], w2_w[:])
-        deal(nc, w2d_s[:], w2_s[:])
+        nc.vector.tensor_copy(*dealt(w2d_s[:], w2_s[:], 16))
+        nc.vector.tensor_copy(*dealt(w2d_w[:], w2_w[:], 4))
 
         def first(t, bank):
             acc = psum.tile([P, J], F32, name="a%d" % t, tag=bank)
@@ -140,55 +144,41 @@ def tile_list_twow_shared_skip_tabled_pl_kernel(
 
         pg = [tile("pg%d" % t, [P, C], F32) for t in range(PACK)]
 
-        a0 = first(0, "bank0")
-        a1 = first(1, "bank1")
-        put_scalar(a0, pw[0], l2, "sa0", "sstage0")
-        put_vector(a1, pw[1], l2, "sa1", "vstage0")
-        b0 = second(0, "bank2")
-        b1 = second(1, "bank3")
-        put_scalar(b0, pv[0], l3, "sb0", "sstage1")
-        put_vector(b1, pv[1], l3, "sb1", "vstage1")
-        nc.gpsimd.tensor_tensor(pg[0][:], pw[0][:], pv[0][:], ADD)
-        nc.gpsimd.tensor_tensor(pg[1][:], pw[1][:], pv[1][:], ADD)
+        put_scalar(first(0, "bank0"), pw[0], l2, "sa0", "sa0")
+        put_vector(first(1, "bank1"), pw[1], l2, "sa1", "vstage0")
+        put_scalar(first(2, "bank2"), pw[2], l2, "sa2", "sa2")
 
-        wbd_w = tile("wbd_w", [P, N], I32)
-        wsd_w = tile("wsd_w", [P, N], I32)
+        lated_w = tile("lated_w", [P, 2 * N], I32)
         lated_s = tile("lated_s", [P, 2 * N], U8)
-        deal(nc, wbd_w[:], wb_w[:])
-        deal(nc, wsd_w[:], ws_w[:])
-        nc.vector.tensor_copy(
-            lated_s[:].rearrange("p (g t m) -> p g m t", g=2, t=PACK),
-            late_s[:].rearrange("p (g m t) -> p g m t", g=2, t=PACK))
+        nc.vector.tensor_copy(*dealt2(lated_w[:], late_w[:], 4))
 
-        a2 = first(2, "bank2")
-        b2 = second(2, "bank1")
-        put_scalar(a2, pw[2], l2, "sa2", "sstage0")
-        put_vector(b2, pv[0], l3, "sb2", "vstage2")
+        put_vector(second(0, "bank3"), pv[0], l3, "sb0", "vstage1")
+        put_scalar(second(2, "bank5"), pv[2], l3, "sb2", "sb2")
+        put_vector(second(1, "bank4"), pv[1], l3, "sb1", "vstage2")
+        for t in (0, 2, 1):
+            nc.gpsimd.tensor_tensor(pg[t][:], pw[t][:], pv[t][:], ADD)
         hid_rows = tile("hid_rows", [P, PACK, O], BF16)
-        for t in (0, 1):
+        nc.scalar.activation(hid_rows[:, 0, :], pg[0][:].indirect(l4[:]), COPY)
+        put_scalar(first(3, "bank0"), pw[0], l2, "sa3", "sa3")
+        nc.vector.tensor_copy(*dealt2(lated_s[:], late_s[:], 16))
+        put_vector(second(3, "bank1"), pv[2], l3, "sb3", "vstage3")
+        for t in (2, 1):
             nc.scalar.activation(hid_rows[:, t, :], pg[t][:].indirect(l4[:]), COPY)
-        nc.gpsimd.tensor_tensor(pg[2][:], pw[2][:], pv[0][:], ADD)
-        a3 = first(3, "bank0")
-        b3 = second(3, "bank3")
+        nc.vector.tensor_tensor(pg[3][:], pw[0][:], pv[2][:], ADD)
 
         acc_p = [psum.tile([P, PACK, HALF], F32, name="p%d" % h) for h in range(2)]
         for h in range(2):
             for t in range(PACK):
                 nc.tensor.matmul_mx(
-                    acc_p[h][:, t, :], lhsT=wsd_w[:, P * t : P * (t + 1)].bitcast(E5M2),
+                    acc_p[h][:, t, :], lhsT=lated_w[:, N + P * t : N + P * (t + 1)].bitcast(E5M2),
                     lhsT_scale=lated_s[:, N + P * t : N + P * (t + 1)],
                     rhs=sx_w[:, 2 * HALF * h : 2 * HALF * (h + 1)].bitcast(E2M1),
                     rhs_scale=sx_s[:, HALF * h : HALF * (h + 1)], start=(t == 0), stop=False)
 
-        put_scalar(a3, pw[1], l2, "sa3", "sstage1")
-        put_vector(b3, pv[1], l3, "sb3", "vstage3")
-        nc.scalar.activation(hid_rows[:, 2, :], pg[2][:].indirect(l4[:]), COPY)
-        nc.vector.tensor_tensor(pg[3][:], pw[1][:], pv[1][:], ADD)
-
-        tzg = [tile("tzg%d" % h, [P, PACK, HALF], F32) for h in range(2)]
+        tzg = tile("tzg", [P, 2, PACK, HALF], F32, tag="pg1")
         for h in range(2):
             for t in range(PACK):
-                nc.scalar.activation(tzg[h][:, t, :], tzt[t][:].indirect(l5[:, HCOL * h : HCOL * (h + 1)]), COPY)
+                nc.scalar.activation(tzg[:, h, t, :], tzt[t][:].indirect(l5[:, HCOL * h : HCOL * (h + 1)]), COPY)
 
         for h in range(2):
             nc.vector.tensor_copy(hid_rows[:, 3, HALF * h : HALF * (h + 1)], pg[3][:].indirect(l4[:, HCOL * h : HCOL * (h + 1)]))
@@ -202,7 +192,7 @@ def tile_list_twow_shared_skip_tabled_pl_kernel(
         for h in range(2):
             for t in range(PACK):
                 nc.tensor.matmul_mx(
-                    acc_p[h][:, t, :], lhsT=wbd_w[:, P * t : P * (t + 1)].bitcast(E5M2),
+                    acc_p[h][:, t, :], lhsT=lated_w[:, P * t : P * (t + 1)].bitcast(E5M2),
                     lhsT_scale=lated_s[:, P * t : P * (t + 1)],
                     rhs=hid_w[h][:].bitcast(E4M3), rhs_scale=hid_s[h][:], start=False, stop=(t == PACK - 1))
 
@@ -213,7 +203,7 @@ def tile_list_twow_shared_skip_tabled_pl_kernel(
         out_rows = out_0.rearrange("(p t) o -> p t o", t=PACK)
         out_words = words(out_1)
         for h in range(2):
-            nc.vector.tensor_tensor(y[h][:], acc_p[h][:], tzg[h][:], ADD)
+            nc.vector.tensor_tensor(y[h][:], acc_p[h][:], tzg[:, h, :, :], ADD)
             nc.sync.dma_start(out_rows[:, :, HALF * h : HALF * (h + 1)], y[h][:])
         nc.scalar.copy(*woven(y_b[0][:], y[0][:]))
         nc.vector.tensor_copy(*woven(y_b[1][:], y[1][:]))

@@ -23,18 +23,13 @@ HALF = O // 2
 HCOL = HALF // 16
 
 
-def load_scales(queue, dst, src):
-    for q in range(4):
+def load_scales(queue, dst, src, quadrants=range(4)):
+    for q in quadrants:
         queue.dma_start(dst[32 * q : 32 * q + 4, :].bitcast(I32), src[0, 4 * q : 4 * q + 4, :].bitcast(I32))
 
 
 def dealt(dst, src, run):
     return (dst.rearrange("p (t c i) -> p c t i", t=PACK, i=run), src.rearrange("p (c i t) -> p c t i", t=PACK, i=run))
-
-
-def dealt2(dst, src, run):
-    return (dst.rearrange("p (g t c i) -> p g c t i", g=2, t=PACK, i=run),
-            src.rearrange("p (g c i t) -> p g c t i", g=2, t=PACK, i=run))
 
 
 def woven(dst, src):
@@ -66,21 +61,23 @@ def tile_list_twow_shared_skip_tabled_pl_kernel(
         xs = tile("xs", [P, T], U8)
         w_s = tile("w_s", [P, R], U8)
         w2_s = tile("w2_s", [P, R], U8)
-        late_s = tile("late_s", [P, 2 * N], U8, tag="vstage3")
+        ws_s = tile("ws_s", [P, N], U8)
+        wb_s = tile("wb_s", [P, N], U8)
         sx_s = tile("sx_s", [P, O], U8)
-        for plane in (w_s, xs, w2_s, late_s, sx_s):
+        for plane in (w_s, xs, w2_s, ws_s, wb_s, sx_s):
             nc.gpsimd.memset(plane[:].bitcast(I32), 0)
-        pw = [tile("pw%d" % i, [P, C], F32) for i in range(3)]
-        pv = [tile("pv%d" % i, [P, C], F32) for i in range(3)]
-        for board in (pw[0], pw[1], pw[2]):
+        pw = [tile("pw%d" % i, [P, C], F32) for i in range(PACK)]
+        pv = [tile("pv%d" % i, [P, C], F32) for i in range(PACK)]
+        for board in pw + pv[:2]:
             nc.vector.memset(board[:], 0.0)
-        for board in (pv[0], pv[2], pv[1]):
+        for board in pv[2:]:
             nc.gpsimd.memset(board[:], 0.0)
 
         xw = tile("xw", [P, T], I32)
         w_w = tile("w_w", [P, 2 * R], U8)
         w2_w = tile("w2_w", [P, R], I32)
-        late_w = tile("late_w", [P, 2 * N], I32, tag="vstage1")
+        ws_w = tile("ws_w", [P, N], I32)
+        wb_w = tile("wb_w", [P, N], I32)
         sx_w = tile("sx_w", [P, 2 * O], U8)
         tzt = [tile("tz%d" % t, [P, E], F32) for t in range(PACK)]
         tz_rows = tz.rearrange("(p t) e -> p t e", t=PACK)
@@ -88,17 +85,18 @@ def tile_list_twow_shared_skip_tabled_pl_kernel(
         nc.sync.dma_start(l1[:], offs)
         nc.sync.dma_start(l2[:], offs2)
         nc.sync.dma_start(l3[:], offs3)
-        load_scales(nc.sync, w_s, w_scales)
+        nc.sync.dma_start(l4[:], offs4)
+        load_scales(nc.sync, w_s, w_scales, range(3))
         nc.sync.dma_start(xw[:], words(xt_words))
+        load_scales(nc.sync, w_s, w_scales, range(3, 4))
         nc.sync.dma_start(w_w[:].bitcast(I32), w_words[0].bitcast(I32))
         load_scales(nc.sync, xs, xt_scales)
-        load_scales(nc.sync, w2_s, w2_scales)
         nc.sync.dma_start(w2_w[:], words(w2_words))
-        nc.sync.dma_start(late_w[:, 0:N], words(wb_words))
-        nc.sync.dma_start(late_w[:, N : 2 * N], words(ws_words))
-        nc.sync.dma_start(l4[:], offs4)
-        load_scales(nc.sync, late_s[:, 0:N], wb_scales)
-        load_scales(nc.sync, late_s[:, N : 2 * N], ws_scales)
+        load_scales(nc.sync, w2_s, w2_scales)
+        load_scales(nc.sync, ws_s, ws_scales)
+        nc.sync.dma_start(ws_w[:], words(ws_words))
+        load_scales(nc.sync, wb_s, wb_scales)
+        nc.sync.dma_start(wb_w[:], words(wb_words))
         nc.sync.dma_start(sx_w[:].bitcast(I32), sx_words[0].bitcast(I32))
         load_scales(nc.sync, sx_s, sx_scales)
         nc.sync.dma_start(l5[:], offs5)
@@ -107,16 +105,12 @@ def tile_list_twow_shared_skip_tabled_pl_kernel(
 
         xg_s = tile("xg_s", [P, J], U8)
         xg_w = tile("xg_w", [P, J], U32)
-        nc.vector.tensor_copy(xg_w[:], xw[:].bitcast(U32).indirect(l1[:]))
-        nc.vector.tensor_copy(xg_s[:], xs[:].indirect(l1[:]))
         wd_w = tile("wd_w", [P, 2 * R], U8)
         wd_s = tile("wd_s", [P, R], U8)
-        nc.vector.tensor_copy(*dealt(wd_w[:].bitcast(U16), w_w[:].bitcast(U16), 8))
+        nc.vector.tensor_copy(xg_w[:], xw[:].bitcast(U32).indirect(l1[:]))
         nc.vector.tensor_copy(*dealt(wd_s[:], w_s[:], 16))
-        w2d_w = tile("w2d_w", [P, R], I32)
-        w2d_s = tile("w2d_s", [P, R], U8)
-        nc.vector.tensor_copy(*dealt(w2d_s[:], w2_s[:], 16))
-        nc.vector.tensor_copy(*dealt(w2d_w[:], w2_w[:], 4))
+        nc.vector.tensor_copy(*dealt(wd_w[:].bitcast(U16), w_w[:].bitcast(U16), 8))
+        nc.vector.tensor_copy(xg_s[:], xs[:].indirect(l1[:]))
 
         def first(t, bank):
             acc = psum.tile([P, J], F32, name="a%d" % t, tag=bank)
@@ -142,43 +136,57 @@ def tile_list_twow_shared_skip_tabled_pl_kernel(
             nc.vector.tensor_copy(st[:], acc[:])
             nc.vector.tensor_copy(board[:].indirect(offsets[:]), st[:])
 
-        pg = [tile("pg%d" % t, [P, C], F32) for t in range(PACK)]
+        pg = [tile("pg%d" % t, [P, C], F32) for t in range(2)]
+        hid_rows = tile("hid_rows", [P, PACK, O], BF16)
 
         put_scalar(first(0, "bank0"), pw[0], l2, "sa0", "sa0")
-        put_vector(first(1, "bank1"), pw[1], l2, "sa1", "vstage0")
+        put_vector(first(1, "bank1"), pw[1], l2, "sa1", "sa1")
         put_scalar(first(2, "bank2"), pw[2], l2, "sa2", "sa2")
+        put_scalar(first(3, "bank3"), pw[3], l2, "sa3", "sa3")
 
-        lated_w = tile("lated_w", [P, 2 * N], I32)
-        lated_s = tile("lated_s", [P, 2 * N], U8)
-        nc.vector.tensor_copy(*dealt2(lated_w[:], late_w[:], 4))
+        w2d_s = tile("w2d_s", [P, R], U8)
+        w2d_w = tile("w2d_w", [P, R], I32)
+        nc.vector.tensor_copy(*dealt(w2d_w[:], w2_w[:], 4))
+        nc.vector.tensor_copy(*dealt(w2d_s[:], w2_s[:], 16))
+        wsd_s = tile("wsd_s", [P, N], U8)
+        wsd_w = tile("wsd_w", [P, N], I32)
+        nc.vector.tensor_copy(*dealt(wsd_s[:], ws_s[:], 16))
+        nc.vector.tensor_copy(*dealt(wsd_w[:], ws_w[:], 4))
 
-        put_vector(second(0, "bank3"), pv[0], l3, "sb0", "vstage1")
-        put_scalar(second(2, "bank5"), pv[2], l3, "sb2", "sb2")
-        put_vector(second(1, "bank4"), pv[1], l3, "sb1", "vstage2")
-        for t in (0, 2, 1):
-            nc.gpsimd.tensor_tensor(pg[t][:], pw[t][:], pv[t][:], ADD)
-        hid_rows = tile("hid_rows", [P, PACK, O], BF16)
-        nc.scalar.activation(hid_rows[:, 0, :], pg[0][:].indirect(l4[:]), COPY)
-        put_scalar(first(3, "bank0"), pw[0], l2, "sa3", "sa3")
-        nc.vector.tensor_copy(*dealt2(lated_s[:], late_s[:], 16))
-        put_vector(second(3, "bank1"), pv[2], l3, "sb3", "vstage3")
-        for t in (2, 1):
+        put_vector(second(0, "bank4"), pv[0], l3, "sb0", "ws_s")
+        put_vector(second(1, "bank5"), pv[1], l3, "sb1", "ws_w")
+        put_scalar(second(2, "bank0"), pv[2], l3, "sb2", "sb2")
+        put_scalar(second(3, "bank2"), pv[3], l3, "sb3", "sb3")
+        pg.append(tile("pg2", [P, C], F32, tag="ws_w"))
+        for t in range(3):
+            nc.vector.tensor_tensor(pg[t][:], pw[t][:], pv[t][:], ADD)
+        for t in range(3):
             nc.scalar.activation(hid_rows[:, t, :], pg[t][:].indirect(l4[:]), COPY)
-        nc.vector.tensor_tensor(pg[3][:], pw[0][:], pv[2][:], ADD)
+
+        wbd_s = tile("wbd_s", [P, N], U8)
+        wbd_w = tile("wbd_w", [P, N], I32)
+        nc.vector.tensor_copy(*dealt(wbd_s[:], wb_s[:], 16))
+        nc.vector.tensor_copy(*dealt(wbd_w[:], wb_w[:], 4))
+        pg.append(tile("pg3", [P, C], F32, tag="wb_w"))
+        nc.vector.tensor_tensor(pg[3][:], pw[3][:], pv[3][:], ADD)
 
         acc_p = [psum.tile([P, PACK, HALF], F32, name="p%d" % h) for h in range(2)]
         for h in range(2):
             for t in range(PACK):
                 nc.tensor.matmul_mx(
-                    acc_p[h][:, t, :], lhsT=lated_w[:, N + P * t : N + P * (t + 1)].bitcast(E5M2),
-                    lhsT_scale=lated_s[:, N + P * t : N + P * (t + 1)],
+                    acc_p[h][:, t, :], lhsT=wsd_w[:, P * t : P * (t + 1)].bitcast(E5M2),
+                    lhsT_scale=wsd_s[:, P * t : P * (t + 1)],
                     rhs=sx_w[:, 2 * HALF * h : 2 * HALF * (h + 1)].bitcast(E2M1),
                     rhs_scale=sx_s[:, HALF * h : HALF * (h + 1)], start=(t == 0), stop=False)
 
-        tzg = tile("tzg", [P, 2, PACK, HALF], F32, tag="pg1")
+        tzg = tile("tzg", [P, 2, PACK, HALF], F32, tag="ws_w")
         for h in range(2):
             for t in range(PACK):
-                nc.scalar.activation(tzg[:, h, t, :], tzt[t][:].indirect(l5[:, HCOL * h : HCOL * (h + 1)]), COPY)
+                picked = tzt[t][:].indirect(l5[:, HCOL * h : HCOL * (h + 1)])
+                if h == 1 and t >= 2:
+                    nc.vector.tensor_copy(tzg[:, h, t, :], picked)
+                else:
+                    nc.scalar.activation(tzg[:, h, t, :], picked, COPY)
 
         for h in range(2):
             nc.vector.tensor_copy(hid_rows[:, 3, HALF * h : HALF * (h + 1)], pg[3][:].indirect(l4[:, HCOL * h : HCOL * (h + 1)]))
@@ -192,8 +200,8 @@ def tile_list_twow_shared_skip_tabled_pl_kernel(
         for h in range(2):
             for t in range(PACK):
                 nc.tensor.matmul_mx(
-                    acc_p[h][:, t, :], lhsT=lated_w[:, P * t : P * (t + 1)].bitcast(E5M2),
-                    lhsT_scale=lated_s[:, P * t : P * (t + 1)],
+                    acc_p[h][:, t, :], lhsT=wbd_w[:, P * t : P * (t + 1)].bitcast(E5M2),
+                    lhsT_scale=wbd_s[:, P * t : P * (t + 1)],
                     rhs=hid_w[h][:].bitcast(E4M3), rhs_scale=hid_s[h][:], start=False, stop=(t == PACK - 1))
 
         y = [tile("y%d" % h, [P, PACK, HALF], F32) for h in range(2)]

@@ -79,8 +79,7 @@ def tile_list_twow_shared_skip_tabled_pl_kernel(
         ws_w = tile("ws_w", [P, N], I32)
         wb_w = tile("wb_w", [P, N], I32)
         sx_w = tile("sx_w", [P, 2 * O], U8)
-        tzt = [tile("tz%d" % t, [P, E], F32) for t in range(PACK)]
-        tz_rows = tz.rearrange("(p t) e -> p t e", t=PACK)
+        tzt = tile("tzt", [P, PACK * E], F32)
 
         nc.sync.dma_start(l1[:], offs)
         nc.sync.dma_start(l2[:], offs2)
@@ -100,8 +99,7 @@ def tile_list_twow_shared_skip_tabled_pl_kernel(
         nc.sync.dma_start(sx_w[:].bitcast(I32), sx_words[0].bitcast(I32))
         load_scales(nc.sync, sx_s, sx_scales)
         nc.sync.dma_start(l5[:], offs5)
-        for t in range(PACK):
-            nc.sync.dma_start(tzt[t][:], tz_rows[:, t, :])
+        nc.sync.dma_start(tzt[:], tz.rearrange("(p t) e -> p (t e)", t=PACK))
 
         xg_s = tile("xg_s", [P, J], U8)
         xg_w = tile("xg_w", [P, J], U32)
@@ -109,8 +107,10 @@ def tile_list_twow_shared_skip_tabled_pl_kernel(
         wd_s = tile("wd_s", [P, R], U8)
         nc.vector.tensor_copy(xg_w[:], xw[:].bitcast(U32).indirect(l1[:]))
         nc.vector.tensor_copy(*dealt(wd_s[:], w_s[:], 16))
-        nc.vector.tensor_copy(*dealt(wd_w[:].bitcast(U16), w_w[:].bitcast(U16), 8))
+        nc.scalar.copy(*dealt(wd_w[:].bitcast(U16), w_w[:].bitcast(U16), 8))
         nc.vector.tensor_copy(xg_s[:], xs[:].indirect(l1[:]))
+        w2d_w = tile("w2d_w", [P, R], U32)
+        nc.scalar.copy(*dealt(w2d_w[:], w2_w[:].bitcast(U32), 4))
 
         def first(t, bank):
             acc = psum.tile([P, J], F32, name="a%d" % t, tag=bank)
@@ -142,11 +142,11 @@ def tile_list_twow_shared_skip_tabled_pl_kernel(
         put_scalar(first(0, "bank0"), pw[0], l2, "sa0", "sa0")
         put_vector(first(1, "bank1"), pw[1], l2, "sa1", "sa1")
         put_scalar(first(2, "bank2"), pw[2], l2, "sa2", "sa2")
-        put_scalar(first(3, "bank3"), pw[3], l2, "sa3", "sa3")
+        sa3 = tile("sa3", [P, J], F32)
+        nc.vector.tensor_copy(sa3[:], first(3, "bank3")[:])
+        nc.scalar.activation(pw[3][:].indirect(l2[:]), sa3[:], COPY)
 
         w2d_s = tile("w2d_s", [P, R], U8)
-        w2d_w = tile("w2d_w", [P, R], I32)
-        nc.vector.tensor_copy(*dealt(w2d_w[:], w2_w[:], 4))
         nc.vector.tensor_copy(*dealt(w2d_s[:], w2_s[:], 16))
         wsd_s = tile("wsd_s", [P, N], U8)
         wsd_w = tile("wsd_w", [P, N], I32)
@@ -182,7 +182,7 @@ def tile_list_twow_shared_skip_tabled_pl_kernel(
         tzg = tile("tzg", [P, 2, PACK, HALF], F32, tag="ws_w")
         for h in range(2):
             for t in range(PACK):
-                picked = tzt[t][:].indirect(l5[:, HCOL * h : HCOL * (h + 1)])
+                picked = tzt[:, E * t : E * (t + 1)].indirect(l5[:, HCOL * h : HCOL * (h + 1)])
                 if h == 1 and t >= 2:
                     nc.vector.tensor_copy(tzg[:, h, t, :], picked)
                 else:

@@ -167,7 +167,7 @@ def tile_list_twow_shared_skip_tabled_pl_kernel(
         wbd_w = tile("wbd_w", [P, N], I32)
         nc.vector.tensor_copy(*dealt(wbd_s[:], wb_s[:], 16))
         nc.vector.tensor_copy(*dealt(wbd_w[:], wb_w[:], 4))
-        pg.append(tile("pg3", [P, C], F32, tag="wb_w"))
+        pg.append(tile("pg3", [P, C], F32, tag="wb_s"))
         nc.vector.tensor_tensor(pg[3][:], pw[3][:], pv[3][:], ADD)
 
         acc_p = [psum.tile([P, PACK, HALF], F32, name="p%d" % h) for h in range(2)]
@@ -183,7 +183,7 @@ def tile_list_twow_shared_skip_tabled_pl_kernel(
         for h in range(2):
             for t in range(PACK):
                 picked = tzt[:, E * t : E * (t + 1)].indirect(l5[:, HCOL * h : HCOL * (h + 1)])
-                if h == 1 and t >= 2:
+                if t >= 2 + h:
                     nc.vector.tensor_copy(tzg[:, h, t, :], picked)
                 else:
                     nc.scalar.activation(tzg[:, h, t, :], picked, COPY)
@@ -193,8 +193,8 @@ def tile_list_twow_shared_skip_tabled_pl_kernel(
         hid_b = [tile("hid_b%d" % h, [P, PACK * HALF], BF16) for h in range(2)]
         hid_w = [tile("hid_w%d" % h, [P, HALF], U32) for h in range(2)]
         hid_s = [tile("hid_s%d" % h, [P, HALF], U8) for h in range(2)]
-        for h in range(2):
-            nc.vector.tensor_copy(*woven(hid_b[h][:], hid_rows[:, :, HALF * h : HALF * (h + 1)]))
+        nc.vector.tensor_copy(*woven(hid_b[0][:], hid_rows[:, :, 0:HALF]))
+        nc.scalar.copy(*woven(hid_b[1][:], hid_rows[:, :, HALF:O]))
         for h in range(2):
             nc.vector.quantize_mx(hid_w[h][:].bitcast(E4M3), hid_s[h][:], hid_b[h][:])
         for h in range(2):

from contextlib import ExitStack

import concourse.mybir as mybir

K, T, J, R, C, O, N, L, E = 512, 1024, 256, 512, 512, 256, 512, 512, 1024
FLOPS = 2 * (2 * K * R * J + R * N * O + L * N * O)

F32 = mybir.dt.float32
BF16 = mybir.dt.bfloat16
I32 = mybir.dt.int32
U32 = mybir.dt.uint32
U16 = mybir.dt.uint16
U8 = mybir.dt.uint8
E4M3 = mybir.dt.float8_e4m3fn_x4
E5M2 = mybir.dt.float8_e5m2_x4
E2M1 = mybir.dt.float4_e2m1fn_x4
ADD = mybir.AluOpType.add
COPY = mybir.ActivationFunctionType.Copy

P = 128
PACK = 4
HALF = O // 2
HCOL = HALF // 16


def load_scales(queue, dst, src, quadrants=range(4)):
    for q in quadrants:
        queue.dma_start(dst[32 * q : 32 * q + 4, :].bitcast(I32), src[0, 4 * q : 4 * q + 4, :].bitcast(I32))


def dealt(dst, src, run):
    return (dst.rearrange("p (t c i) -> p c t i", t=PACK, i=run), src.rearrange("p (c i t) -> p c t i", t=PACK, i=run))


def woven(dst, src):
    return dst.rearrange("p (c i t) -> p c t i", i=4, t=PACK), src.rearrange("p t (c i) -> p c t i", i=4)


def tile_list_twow_shared_skip_tabled_pl_kernel(
    tc, xt_words, xt_scales, w_words, w_scales, w2_words, w2_scales, wb_words, wb_scales,
    sx_words, sx_scales, ws_words, ws_scales, tz, offs, offs2, offs3, offs4, offs5, out_0, out_1, out_2,
):
    nc = tc.nc
    with ExitStack() as ctx:
        lists = ctx.enter_context(tc.tile_pool(name="lists", bufs=1))
        sb = ctx.enter_context(tc.tile_pool(name="sb", bufs=1))
        psum = ctx.enter_context(tc.psum_pool(name="psum", bufs=1))

        def tile(name, shape, dtype, tag=None):
            return sb.tile(shape, dtype, name=name, tag=tag or name, align_bytes=64)

        def words(src):
            return src[0].rearrange("p c r -> p (c r)").bitcast(I32)

        l1 = lists.tile([P, J // 16], U16, name="l1")
        l2 = lists.tile([P, J // 16], U16, name="l2")
        l3 = lists.tile([P, J // 16], U16, name="l3")
        l4 = lists.tile([P, O // 16], U16, name="l4")
        l5 = lists.tile([P, O // 16], U16, name="l5")

        xs = tile("xs", [P, T], U8)
        w_s = tile("w_s", [P, R], U8)
        w2_s = tile("w2_s", [P, R], U8)
        ws_s = tile("ws_s", [P, N], U8)
        wb_s = tile("wb_s", [P, N], U8)
        sx_s = tile("sx_s", [P, O], U8)
        for plane in (w_s, xs, w2_s, ws_s, wb_s, sx_s):
            nc.gpsimd.memset(plane[:].bitcast(I32), 0)
        pw = [tile("pw%d" % i, [P, C], F32) for i in range(PACK)]
        pv = [tile("pv%d" % i, [P, C], F32) for i in range(PACK)]
        for board in pw + pv[:2]:
            nc.vector.memset(board[:], 0.0)
        for board in pv[2:]:
            nc.gpsimd.memset(board[:], 0.0)

        xw = tile("xw", [P, T], I32)
        w_w = tile("w_w", [P, 2 * R], U8)
        w2_w = tile("w2_w", [P, R], I32)
        ws_w = tile("ws_w", [P, N], I32)
        wb_w = tile("wb_w", [P, N], I32)
        sx_w = tile("sx_w", [P, 2 * O], U8)
        tzt = tile("tzt", [P, PACK * E], F32)

        nc.sync.dma_start(l1[:], offs)
        nc.sync.dma_start(l2[:], offs2)
        nc.sync.dma_start(l3[:], offs3)
        nc.sync.dma_start(l4[:], offs4)
        load_scales(nc.sync, w_s, w_scales, range(3))
        nc.sync.dma_start(xw[:], words(xt_words))
        load_scales(nc.sync, w_s, w_scales, range(3, 4))
        nc.sync.dma_start(w_w[:].bitcast(I32), w_words[0].bitcast(I32))
        load_scales(nc.sync, xs, xt_scales)
        nc.sync.dma_start(w2_w[:], words(w2_words))
        load_scales(nc.sync, w2_s, w2_scales)
        load_scales(nc.sync, ws_s, ws_scales)
        nc.sync.dma_start(ws_w[:], words(ws_words))
        load_scales(nc.sync, wb_s, wb_scales)
        nc.sync.dma_start(wb_w[:], words(wb_words))
        nc.sync.dma_start(sx_w[:].bitcast(I32), sx_words[0].bitcast(I32))
        load_scales(nc.sync, sx_s, sx_scales)
        nc.sync.dma_start(l5[:], offs5)
        nc.sync.dma_start(tzt[:], tz.rearrange("(p t) e -> p (t e)", t=PACK))

        xg_s = tile("xg_s", [P, J], U8)
        xg_w = tile("xg_w", [P, J], U32)
        wd_w = tile("wd_w", [P, 2 * R], U8)
        wd_s = tile("wd_s", [P, R], U8)
        nc.vector.tensor_copy(xg_w[:], xw[:].bitcast(U32).indirect(l1[:]))
        nc.vector.tensor_copy(*dealt(wd_s[:], w_s[:], 16))
        nc.scalar.copy(*dealt(wd_w[:].bitcast(U16), w_w[:].bitcast(U16), 8))
        nc.vector.tensor_copy(xg_s[:], xs[:].indirect(l1[:]))
        w2d_w = tile("w2d_w", [P, R], U32)
        nc.scalar.copy(*dealt(w2d_w[:], w2_w[:].bitcast(U32), 4))

        def first(t, bank):
            acc = psum.tile([P, J], F32, name="a%d" % t, tag=bank)
            nc.tensor.matmul_mx(
                acc[:], lhsT=wd_w[:, 2 * P * t : 2 * P * (t + 1)].bitcast(E2M1), lhsT_scale=wd_s[:, P * t : P * (t + 1)],
                rhs=xg_w[:].bitcast(E4M3), rhs_scale=xg_s[:], start=True, stop=True)
            return acc

        def second(t, bank):
            acc = psum.tile([P, J], F32, name="b%d" % t, tag=bank)
            nc.tensor.matmul_mx(
                acc[:], lhsT=w2d_w[:, P * t : P * (t + 1)].bitcast(E5M2), lhsT_scale=w2d_s[:, P * t : P * (t + 1)],
                rhs=xg_w[:].bitcast(E4M3), rhs_scale=xg_s[:], start=True, stop=True)
            return acc

        def put_scalar(acc, board, offsets, name, tag):
            st = tile(name, [P, J], F32, tag=tag)
            nc.scalar.activation(st[:], acc[:], COPY)
            nc.scalar.activation(board[:].indirect(offsets[:]), st[:], COPY)

        def put_vector(acc, board, offsets, name, tag):
            st = tile(name, [P, J], F32, tag=tag)
            nc.vector.tensor_copy(st[:], acc[:])
            nc.vector.tensor_copy(board[:].indirect(offsets[:]), st[:])

        pg = [tile("pg%d" % t, [P, C], F32) for t in range(2)]
        hid_rows = tile("hid_rows", [P, PACK, O], BF16)

        put_scalar(first(0, "bank0"), pw[0], l2, "sa0", "sa0")
        put_vector(first(1, "bank1"), pw[1], l2, "sa1", "sa1")
        put_scalar(first(2, "bank2"), pw[2], l2, "sa2", "sa2")
        sa3 = tile("sa3", [P, J], F32)
        nc.vector.tensor_copy(sa3[:], first(3, "bank3")[:])
        nc.scalar.activation(pw[3][:].indirect(l2[:]), sa3[:], COPY)

        w2d_s = tile("w2d_s", [P, R], U8)
        nc.vector.tensor_copy(*dealt(w2d_s[:], w2_s[:], 16))
        wsd_s = tile("wsd_s", [P, N], U8)
        wsd_w = tile("wsd_w", [P, N], I32)
        nc.vector.tensor_copy(*dealt(wsd_s[:], ws_s[:], 16))
        nc.vector.tensor_copy(*dealt(wsd_w[:], ws_w[:], 4))

        put_vector(second(0, "bank4"), pv[0], l3, "sb0", "ws_s")
        put_vector(second(1, "bank5"), pv[1], l3, "sb1", "ws_w")
        put_scalar(second(2, "bank0"), pv[2], l3, "sb2", "sb2")
        put_scalar(second(3, "bank2"), pv[3], l3, "sb3", "sb3")
        pg.append(tile("pg2", [P, C], F32, tag="ws_w"))
        for t in range(3):
            nc.vector.tensor_tensor(pg[t][:], pw[t][:], pv[t][:], ADD)
        for t in range(3):
            nc.scalar.activation(hid_rows[:, t, :], pg[t][:].indirect(l4[:]), COPY)

        wbd_s = tile("wbd_s", [P, N], U8)
        wbd_w = tile("wbd_w", [P, N], I32)
        nc.vector.tensor_copy(*dealt(wbd_s[:], wb_s[:], 16))
        nc.vector.tensor_copy(*dealt(wbd_w[:], wb_w[:], 4))
        pg.append(tile("pg3", [P, C], F32, tag="wb_s"))
        nc.vector.tensor_tensor(pg[3][:], pw[3][:], pv[3][:], ADD)

        acc_p = [psum.tile([P, PACK, HALF], F32, name="p%d" % h) for h in range(2)]
        for h in range(2):
            for t in range(PACK):
                nc.tensor.matmul_mx(
                    acc_p[h][:, t, :], lhsT=wsd_w[:, P * t : P * (t + 1)].bitcast(E5M2),
                    lhsT_scale=wsd_s[:, P * t : P * (t + 1)],
                    rhs=sx_w[:, 2 * HALF * h : 2 * HALF * (h + 1)].bitcast(E2M1),
                    rhs_scale=sx_s[:, HALF * h : HALF * (h + 1)], start=(t == 0), stop=False)

        tzg = tile("tzg", [P, 2, PACK, HALF], F32, tag="ws_w")
        for h in range(2):
            for t in range(PACK):
                picked = tzt[:, E * t : E * (t + 1)].indirect(l5[:, HCOL * h : HCOL * (h + 1)])
                if t >= 2 + h:
                    nc.vector.tensor_copy(tzg[:, h, t, :], picked)
                else:
                    nc.scalar.activation(tzg[:, h, t, :], picked, COPY)

        for h in range(2):
            nc.vector.tensor_copy(hid_rows[:, 3, HALF * h : HALF * (h + 1)], pg[3][:].indirect(l4[:, HCOL * h : HCOL * (h + 1)]))
        hid_b = [tile("hid_b%d" % h, [P, PACK * HALF], BF16) for h in range(2)]
        hid_w = [tile("hid_w%d" % h, [P, HALF], U32) for h in range(2)]
        hid_s = [tile("hid_s%d" % h, [P, HALF], U8) for h in range(2)]
        nc.vector.tensor_copy(*woven(hid_b[0][:], hid_rows[:, :, 0:HALF]))
        nc.scalar.copy(*woven(hid_b[1][:], hid_rows[:, :, HALF:O]))
        for h in range(2):
            nc.vector.quantize_mx(hid_w[h][:].bitcast(E4M3), hid_s[h][:], hid_b[h][:])
        for h in range(2):
            for t in range(PACK):
                nc.tensor.matmul_mx(
                    acc_p[h][:, t, :], lhsT=wbd_w[:, P * t : P * (t + 1)].bitcast(E5M2),
                    lhsT_scale=wbd_s[:, P * t : P * (t + 1)],
                    rhs=hid_w[h][:].bitcast(E4M3), rhs_scale=hid_s[h][:], start=False, stop=(t == PACK - 1))

        y = [tile("y%d" % h, [P, PACK, HALF], F32) for h in range(2)]
        y_b = [tile("y_b%d" % h, [P, PACK * HALF], BF16) for h in range(2)]
        y_w = [tile("y_w%d" % h, [P, HALF], I32) for h in range(2)]
        y_s = tile("y_s", [P, O], U8)
        out_rows = out_0.rearrange("(p t) o -> p t o", t=PACK)
        out_words = words(out_1)
        for h in range(2):
            nc.vector.tensor_tensor(y[h][:], acc_p[h][:], tzg[:, h, :, :], ADD)
            nc.sync.dma_start(out_rows[:, :, HALF * h : HALF * (h + 1)], y[h][:])
        nc.scalar.copy(*woven(y_b[0][:], y[0][:]))
        nc.vector.tensor_copy(*woven(y_b[1][:], y[1][:]))
        for h in range(2):
            nc.vector.quantize_mx(y_w[h][:].bitcast(E4M3), y_s[:, HALF * h : HALF * (h + 1)], y_b[h][:])
            nc.sync.dma_start(out_words[:, HALF * h : HALF * (h + 1)], y_w[h][:])
        for q in range(4):
            queue = nc.scalar if q % 2 == 0 else nc.sync
            queue.dma_start(out_2[0, 4 * q : 4 * q + 4, :].bitcast(I32), y_s[32 * q : 32 * q + 4, :].bitcast(I32))
